import numpy as np, ml_dtypes
CORES = [2,6,26,30,66,70,74,78,82,86]
N = 10
F, TK = 128, 512
def setup_inputs(rng):
    return {"x": rng.standard_normal((N, 128, N * TK), dtype=np.float32).astype(ml_dtypes.bfloat16), "w": rng.standard_normal((N, 128, F), dtype=np.float32).astype(ml_dtypes.bfloat16)}
def setup_inputs_big(rng):
    d = setup_inputs(rng)
    for k in ("x", "w"): d[k] = (d[k].astype(np.float32) * 1024.0).astype(d[k].dtype)
    return d
def setup_inputs_small(rng):
    d = setup_inputs(rng)
    for k in ("x", "w"): d[k] = (d[k].astype(np.float32) * (1 / 1024.0)).astype(d[k].dtype)
    return d
def reference(x, w):
    X, W = x.astype(np.float64), w.astype(np.float64)
    y = np.zeros((N, F, N * TK))
    for r in range(N):
        for j in range(N):
            y[r][:, TK * j:TK * j + TK] = W[r].T @ X[j][:, TK * r:TK * r + TK]
    return {"y": y.astype(ml_dtypes.bfloat16 if x.dtype != np.float64 else np.float64)}

from concourse.bass import DstId, RemoteDMATransfer

N, TK, NB = 10, 512, 8
OFFLOAD = True
PEER_ROUND = 2
VIA_LAG = 1.2

SCRATCH = {
    "xs": ("sbuf", [128, N * TK], "bfloat16"),
    "land": ("sbuf", [128, N * TK], "bfloat16"),
    "ys": ("sbuf", [128, N * TK], "bfloat16"),
    "ws": ("sbuf", [128, 128], "bfloat16"),
    "hold": ("sbuf", [128, 4 * TK], "bfloat16"),
}
for _b in range(NB):
    SCRATCH["ps%d" % _b] = ("psum", [128, TK], "float32")
SEMAPHORES = (["wl", "snt", "st_a", "st_b"] + ["ld%d" % i for i in range(N)] + ["hin%d" % i for i in range(4)]
              + ["arr%d" % i for i in range(N)] + ["mm%d" % i for i in range(N)] + ["cp%d" % i for i in range(N)])

_CACHE = {}


def _bits(mask):
    return [e for e in range(mask.bit_length()) if (mask >> e) & 1]


def _mask(engs):
    return sum(1 << e for e in engs)


def _perms(items):
    if not items:
        return [[]]
    return [[a] + rest for i, a in enumerate(items) for rest in _perms(items[:i] + items[i + 1:])]


def _latin(ok, chosen, chips, start):
    if len(chosen) == len(chips) - 1:
        return chosen
    for i in range(start, len(ok)):
        if all(ok[i][a] != e[a] for e in chosen for a in chips):
            got = _latin(ok, chosen + [ok[i]], chips, i + 1)
            if got:
                return got
    return None


def _rounds(chips, topo):
    def links(a, b):
        if topo.same_plane(a, b):
            return [("out", a), ("in", b)]
        if topo.mates(a, b):
            return [("mate", a)]
        m = [k for k in range(topo.CHIPS) if topo.mates(a, k)][0]
        return [("mate", a), ("out", m), ("in", b)]
    ders = []
    for p in _perms(chips):
        if all(a != b for a, b in zip(chips, p)):
            load = {}
            for a, b in zip(chips, p):
                for l in links(a, b):
                    load[l] = load.get(l, 0) + 1
            ders.append((max(load.values()), dict(zip(chips, p))))
    for bound in range(1, len(chips) + 1):
        got = _latin([d for c, d in ders if c <= bound], [], chips, 0)
        if got:
            return got
    return None


def _plan(T, topo):
    if "plan" in _CACHE:
        return _CACHE["plan"]
    cores = list(T.cores)
    chips, members = [], {}
    for r, c in enumerate(cores):
        if topo.chip(c) not in members:
            members[topo.chip(c)] = []
            chips.append(topo.chip(c))
        members[topo.chip(c)].append(r)
    rounds = _rounds(chips, topo)
    prog = {}
    arr = {}
    for s, c in enumerate(cores):
        a = topo.chip(c)
        idle = [h for h in range(topo.CHIPS * topo.CORES_PER_CHIP)
                if topo.chip(h) == a and topo.die(h) == topo.die(c) and h not in cores
                and all(topo.may_write(h, d) for d in cores)]
        h = idle[0] if (OFFLOAD and idle) else None
        peers = [r for r in members[a] if r != s]
        prog[c] = []
        if h is not None:
            prog[h] = []
        for k, rd in enumerate(rounds):
            dsts = members[rd[a]]
            low = _bits(topo.mask(c, cores[dsts[0]]))
            near = h if h is not None else (cores[peers[0]] if peers else None)
            high = [e for e in _bits(topo.mask(c, near)) if e not in low] if near is not None else []
            waits = [("ld%d" % chips.index(rd[a]), 16)]
            trs = []
            ride = peers if k == PEER_ROUND else []
            if h is not None and len(dsts) == 2:
                d0, d1 = dsts[k % 2], dsts[1 - k % 2]
                trs.append((cores[d0], "xs", d0 * TK, "land", s * TK, "arr%d" % s, low))
                arr[(d0, s)] = (len(low), k)
                up = high[:len(high) // 2] if ride else high
                high = high[len(high) // 2:]
                slot = len(prog[h])
                trs.append((h, "xs", d1 * TK, "hold", slot * TK, "hin%d" % slot, up))
                out = _bits(topo.mask(h, cores[d1]))
                prog[h].append(([("hin%d" % slot, len(up))],
                                [(cores[d1], "hold", slot * TK, "land", s * TK, "arr%d" % s, out)]))
                arr[(d1, s)] = (len(out), k + VIA_LAG)
            else:
                per = len(low) // len(dsts)
                for i, d in enumerate(dsts):
                    trs.append((cores[d], "xs", d * TK, "land", s * TK, "arr%d" % s, low[i * per:(i + 1) * per]))
                    arr[(d, s)] = (per, k)
                high = high[::2]
            for p in ride:
                waits.append(("ld%d" % chips.index(a), 16))
                trs.append((cores[p], "xs", p * TK, "land", s * TK, "arr%d" % s, high))
                arr[(p, s)] = (len(high), k - 0.5)
            prog[c].append((waits, trs))
    _CACHE["plan"] = (chips, members, rounds, prog, arr)
    return _CACHE["plan"]


def rank_program(g, core, T, topo):
    chips, members, rounds, prog, arr = _plan(T, topo)
    S = T.sem
    rank = T.rank_of(core)
    queues = [g.sync, g.scalar]

    if rank is not None:
        me = topo.chip(core)
        seq = [rd[me] for rd in rounds]
        seq.insert(PEER_ROUND, me)
        for i, ch in enumerate(seq):
            lo, hi = TK * min(members[ch]), TK * (max(members[ch]) + 1)
            queues[i % 2].dma_start(T.xs[:, lo:hi], T.x[:, lo:hi]).then_inc(S["ld%d" % chips.index(ch)], 16)
            if i == 1:
                queues[1].dma_start(T.ws[:], T.w[:]).then_inc(S.wl, 16)

    total = 0
    for waits, trs in prog.get(core, []):
        for name, cnt in waits:
            g.wait_ge(S[name], cnt)
        fused = []
        for dc, sb, s0, db, d0, sem, engs in trs:
            rid, pid, _se = topo.addr(dc)
            fused.append(RemoteDMATransfer(dst_ids=[DstId(rid=rid, pnc=pid)], dma_engine_mask=_mask(engs),
                                           remote_sem=S[sem], src=T[sb][:, s0:s0 + TK], dst=T[db][:, d0:d0 + TK]))
            total += len(engs)
        g.remote_dma_fused(fused, local_sem=S.snt)
    if total:
        g.wait_ge(S.snt, total)
    if rank is None:
        return

    order = [rank] + sorted([j for j in range(N) if j != rank], key=lambda j: (arr[(rank, j)][1], j))
    g.tensor.wait_ge(S.wl, 16)
    for i, j in enumerate(order):
        if j == rank:
            g.tensor.wait_ge(S["ld%d" % chips.index(me)], 16)
            rhs = T.xs[:, j * TK:(j + 1) * TK]
        else:
            g.tensor.wait_ge(S["arr%d" % j], arr[(rank, j)][0])
            rhs = T.land[:, j * TK:(j + 1) * TK]
        if i >= NB:
            g.tensor.wait_ge(S["cp%d" % order[i - NB]], 1)
        g.tensor.matmul(T["ps%d" % (i % NB)][:], T.ws[:], rhs, start=True, stop=True).then_inc(S["mm%d" % j], 1)
        g.vector.wait_ge(S["mm%d" % j], 1)
        g.vector.tensor_copy(T.ys[:, j * TK:(j + 1) * TK], T["ps%d" % (i % NB)][:]).then_inc(S["cp%d" % j], 1)

    groups = sorted([members[ch] for ch in chips], key=lambda m: max(order.index(j) for j in m))
    pieces = groups[:-1] + [[j] for j in sorted(groups[-1], key=order.index)]
    count = [0, 0]
    for i, m in enumerate(pieces):
        q = queues[i % 2]
        for j in m:
            q.wait_ge(S["cp%d" % j], 1)
        lo, hi = TK * min(m), TK * (max(m) + 1)
        q.dma_start(T.y[:, lo:hi], T.ys[:, lo:hi]).then_inc(S.st_a if i % 2 == 0 else S.st_b, 16)
        count[i % 2] += 16
    g.sync.wait_ge(S.st_a, count[0])
    g.scalar.wait_ge(S.st_b, count[1])
